import numpy as np
import ml_dtypes

BF16 = ml_dtypes.bfloat16


def bf(x):
    return np.asarray(x, np.float32).astype(BF16)


def f32(x):
    return np.asarray(x, np.float32)


def f64(x):
    return np.asarray(x).astype(np.float64)


def striped(idx):
    return np.tile(idx.reshape(-1, 16).T, (8, 1))


def rows(idx, k):
    return np.tile(idx, (k, 1))


def look(tab, idx):
    return np.take_along_axis(f64(tab), rows(idx, len(tab)), axis=1)


K, S, V, N = 256, 2048, 512, 512


def silu(v):
    return v / (1.0 + np.exp(-v))


def setup_inputs():
    return {"tab": f32(np.random.standard_normal((2, K, S))), "y": f32(np.random.standard_normal((K, V))), "offs": striped(np.random.permutation(S)[:N])}


def reference(tab, y, offs):
    idx = offs[:16].T.reshape(-1)
    x = (look(tab[0], idx) + f64(y)) * (silu(look(tab[1], idx)))
    return x

@@ -1,0 +1,42 @@
+import concourse.mybir as mybir
+
+F32 = mybir.dt.float32
+U16 = mybir.dt.uint16
+ADD = mybir.AluOpType.add
+MULT = mybir.AluOpType.mult
+SILU = mybir.ActivationFunctionType.Silu
+
+P = 128
+
+
+def tile_lookup_vg_addsilu_out_kernel(tc, tab, y, offs, out):
+    nc = tc.nc
+    rows, places = tab.shape[1], tab.shape[2]
+    n = y.shape[1]
+    blocks = rows // P
+
+    with tc.tile_pool(name="held", bufs=1) as held:
+        offsets = held.tile([P, n // 16], U16, name="offsets")
+        nc.sync.dma_start(offsets[:], offs)
+
+        gates, values, streams = [], [], []
+        for b in range(blocks):
+            block = slice(b * P, (b + 1) * P)
+            gate = held.tile([P, places], F32, name=f"gate{b}")
+            nc.sync.dma_start(gate[:], tab[1, block, :])
+            stream = held.tile([P, n], F32, name=f"stream{b}")
+            nc.sync.dma_start(stream[:], y[block, :])
+            value = held.tile([P, places], F32, name=f"value{b}")
+            nc.sync.dma_start(value[:], tab[0, block, :])
+            gates.append(gate)
+            streams.append(stream)
+            values.append(value)
+
+        for b in range(blocks):
+            opened = held.tile([P, n], F32, name=f"opened{b}")
+            nc.scalar.activation(opened[:], gates[b][:].indirect(offsets[:]), SILU)
+            summed = held.tile([P, n], F32, name=f"summed{b}")
+            nc.vector.tensor_tensor(summed[:], values[b][:].indirect(offsets[:]), streams[b][:], ADD)
+            product = held.tile([P, n], F32, name=f"product{b}")
+            nc.vector.tensor_tensor(product[:], summed[:], opened[:], MULT)
+            nc.sync.dma_start(out[b * P : (b + 1) * P, :], product[:])

@@ -7,6 +7,7 @@ MULT = mybir.AluOpType.mult
 SILU = mybir.ActivationFunctionType.Silu
 
 P = 128
+PIECES = 2
 
 
 def tile_lookup_vg_addsilu_out_kernel(tc, tab, y, offs, out):
@@ -35,8 +36,11 @@ def tile_lookup_vg_addsilu_out_kernel(tc, tab, y, offs, out):
         for b in range(blocks):
             opened = held.tile([P, n], F32, name=f"opened{b}")
             nc.scalar.activation(opened[:], gates[b][:].indirect(offsets[:]), SILU)
-            summed = held.tile([P, n], F32, name=f"summed{b}")
-            nc.vector.tensor_tensor(summed[:], values[b][:].indirect(offsets[:]), streams[b][:], ADD)
-            product = held.tile([P, n], F32, name=f"product{b}")
-            nc.vector.tensor_tensor(product[:], summed[:], opened[:], MULT)
-            nc.sync.dma_start(out[b * P : (b + 1) * P, :], product[:])
+            for h in range(PIECES):
+                part = slice(h * n // PIECES, (h + 1) * n // PIECES)
+                part_offsets = offsets[:, h * n // 16 // PIECES : (h + 1) * n // 16 // PIECES]
+                summed = held.tile([P, n // PIECES], F32, name=f"summed{b}_{h}")
+                nc.vector.tensor_tensor(summed[:], values[b][:].indirect(part_offsets), streams[b][:, part], ADD)
+                product = held.tile([P, n // PIECES], F32, name=f"product{b}_{h}")
+                nc.vector.tensor_tensor(product[:], summed[:], opened[:, part], MULT)
+                nc.sync.dma_start(out[b * P : (b + 1) * P, part], product[:])

@@ -18,19 +18,19 @@ def tile_lookup_vg_addsilu_out_kernel(tc, tab, y, offs, out):
 
     with tc.tile_pool(name="held", bufs=1) as held:
         offsets = held.tile([P, n // 16], U16, name="offsets")
-        nc.sync.dma_start(offsets[:], offs)
+        streams = held.tile([P, blocks, n], F32, name="streams")
 
-        gates, values, streams = [], [], []
+        gates, values = [], []
         for b in range(blocks):
             block = slice(b * P, (b + 1) * P)
             gate = held.tile([P, places], F32, name=f"gate{b}")
             nc.sync.dma_start(gate[:], tab[1, block, :])
-            stream = held.tile([P, n], F32, name=f"stream{b}")
-            nc.sync.dma_start(stream[:], y[block, :])
+            if b == 0:
+                nc.sync.dma_start(offsets[:], offs)
+                nc.sync.dma_start(streams[:], y.rearrange("(b p) n -> p b n", p=P))
             value = held.tile([P, places], F32, name=f"value{b}")
             nc.sync.dma_start(value[:], tab[0, block, :])
             gates.append(gate)
-            streams.append(stream)
             values.append(value)
 
         for b in range(blocks):
@@ -40,7 +40,7 @@ def tile_lookup_vg_addsilu_out_kernel(tc, tab, y, offs, out):
                 part = slice(h * n // PIECES, (h + 1) * n // PIECES)
                 part_offsets = offsets[:, h * n // 16 // PIECES : (h + 1) * n // 16 // PIECES]
                 summed = held.tile([P, n // PIECES], F32, name=f"summed{b}_{h}")
-                nc.vector.tensor_tensor(summed[:], values[b][:].indirect(part_offsets), streams[b][:, part], ADD)
+                nc.vector.tensor_tensor(summed[:], values[b][:].indirect(part_offsets), streams[:, b, part], ADD)
                 product = held.tile([P, n // PIECES], F32, name=f"product{b}_{h}")
                 nc.vector.tensor_tensor(product[:], summed[:], opened[:, part], MULT)
                 nc.sync.dma_start(out[b * P : (b + 1) * P, part], product[:])

import concourse.mybir as mybir

F32 = mybir.dt.float32
U16 = mybir.dt.uint16
ADD = mybir.AluOpType.add
MULT = mybir.AluOpType.mult
SILU = mybir.ActivationFunctionType.Silu

P = 128
PIECES = 2


def tile_lookup_vg_addsilu_out_kernel(tc, tab, y, offs, out):
    nc = tc.nc
    rows, places = tab.shape[1], tab.shape[2]
    n = y.shape[1]
    blocks = rows // P

    with tc.tile_pool(name="held", bufs=1) as held:
        offsets = held.tile([P, n // 16], U16, name="offsets")
        streams = held.tile([P, blocks, n], F32, name="streams")

        gates, values = [], []
        for b in range(blocks):
            block = slice(b * P, (b + 1) * P)
            gate = held.tile([P, places], F32, name=f"gate{b}")
            nc.sync.dma_start(gate[:], tab[1, block, :])
            if b == 0:
                nc.sync.dma_start(offsets[:], offs)
                nc.sync.dma_start(streams[:], y.rearrange("(b p) n -> p b n", p=P))
            value = held.tile([P, places], F32, name=f"value{b}")
            nc.sync.dma_start(value[:], tab[0, block, :])
            gates.append(gate)
            values.append(value)

        for b in range(blocks):
            opened = held.tile([P, n], F32, name=f"opened{b}")
            nc.scalar.activation(opened[:], gates[b][:].indirect(offsets[:]), SILU)
            for h in range(PIECES):
                part = slice(h * n // PIECES, (h + 1) * n // PIECES)
                part_offsets = offsets[:, h * n // 16 // PIECES : (h + 1) * n // 16 // PIECES]
                summed = held.tile([P, n // PIECES], F32, name=f"summed{b}_{h}")
                nc.vector.tensor_tensor(summed[:], values[b][:].indirect(part_offsets), streams[:, b, part], ADD)
                product = held.tile([P, n // PIECES], F32, name=f"product{b}_{h}")
                nc.vector.tensor_tensor(product[:], summed[:], opened[:, part], MULT)
                nc.sync.dma_start(out[b * P : (b + 1) * P, part], product[:])
